import numpy as np
import ml_dtypes


def mxq(x, axis, fmt="e4m3"):
    dtype, down = {"e4m3": (ml_dtypes.float8_e4m3fn, 7), "e5m2": (ml_dtypes.float8_e5m2, 14)}[fmt]
    v = np.moveaxis(np.asarray(x, np.float32).astype(ml_dtypes.bfloat16).astype(np.float64), axis, -1)
    blocks = v.reshape(v.shape[:-1] + (-1, 32))
    amax = np.abs(blocks).max(-1, keepdims=True)
    byte = np.maximum(np.where(amax > 0, np.frexp(amax)[1] - 1 + 127, 0) - down, 1)
    scale = np.exp2(byte - 127.0)
    codes = (blocks / scale).astype(np.float32).astype(dtype).astype(np.float64)
    return np.moveaxis((codes * scale).reshape(v.shape), -1, axis)


WIDE = False


def mx_kscale(k):
    if not WIDE:
        return np.ones(k)
    levels = np.array([10, -10, 5, -5, 0])
    if k % 512:
        return np.exp2(np.random.permutation(np.resize(levels, k // 32))).repeat(32)
    a = np.empty((k // 512, 16))
    for p in range(k // 512):
        a[p, :8] = np.random.permutation(np.resize(levels, 8))
        for g in range(8):
            far = levels[np.abs(levels - a[p, g]) >= 10]
            a[p, g + 8] = far[np.random.randint(len(far))]
    return np.exp2(a.ravel()).repeat(32)


BF16 = ml_dtypes.bfloat16


def bf(x):
    return np.asarray(x, np.float32).astype(BF16)


def f64(x):
    return np.asarray(x).astype(np.float64)


E2M1 = np.array([0.0, 0.5, 1.0, 1.5, 2.0, 3.0, 4.0, 6.0, -0.0, -0.5, -1.0, -1.5, -2.0, -3.0, -4.0, -6.0])


def pack_weight(w, fmt):
    k, n = w.shape
    w = f64(bf(w)).reshape(k // 32, 32, n)
    amax = np.abs(w).max(1)
    if fmt == "e4m3":
        byte = np.frexp(amax)[1] - 1 + 127 - 7
    else:
        mant, ex = np.frexp(amax / 6.0)
        byte = np.where(mant > 0.5, ex, ex - 1) + 127
    byte = np.clip(np.where(amax > 0, byte, 1), 1, 254)
    scaled = (w * np.exp2(127.0 - byte)[:, None, :]).reshape(k, n).astype(np.float32)
    by_word = np.ascontiguousarray(scaled.reshape(k // 512, 128, 4, n).transpose(0, 1, 3, 2))
    if fmt == "e4m3":
        words = by_word.astype(ml_dtypes.float8_e4m3fn).view(np.uint8)
    else:
        c = by_word.astype(ml_dtypes.float4_e2m1fn).view(np.uint8) & 0xF
        words = c[..., 0::2] | (c[..., 1::2] << 4)
    return np.ascontiguousarray(words), np.ascontiguousarray(byte.astype(np.uint8).reshape(k // 512, 16, n))


def unpack_weight(words, scales, fmt):
    g, p, n, _ = words.shape
    if fmt == "e4m3":
        vals = np.ascontiguousarray(words).view(ml_dtypes.float8_e4m3fn).astype(np.float64)
    else:
        nib = np.empty((g, p, n, 4), np.uint8)
        nib[..., 0::2] = words & 0xF
        nib[..., 1::2] = words >> 4
        vals = E2M1[nib]
    vals = vals * np.repeat(np.exp2(scales.astype(np.float64) - 127.0), 8, axis=1)[..., None]
    return vals.transpose(0, 1, 3, 2).reshape(g * 512, n)
def pack4(w):
    words, scales = pack_weight(w, "e2m1")
    return words.reshape(words.shape[0], 128, -1), scales


def unpack4(words, scales):
    return unpack_weight(words.reshape(words.shape[0], 128, -1, 2), scales, "e2m1")


R, T, A, F, P = 1536, 2048, 1024, 1536, 512


def setup_inputs():
    s, f = mx_kscale(T), mx_kscale(F)
    t = mx_kscale(A)
    h = np.random.standard_normal((F, A)) * f[:, None] / t
    x = np.random.standard_normal((F, P)) / (np.sqrt(F) * A ** 0.25) / f[:, None]
    h_words, h_scales = pack4(h)
    x_words, x_scales = pack4(x)
    return {"d": bf(np.random.standard_normal((R, T)) / A ** 0.25 * s),
            "b": bf(np.random.standard_normal((A, T)) / np.sqrt(T) / s * t[:, None]),
            "gap": bf(np.random.uniform(0.5, 2.0, T)),
            "h_words": h_words, "h_scales": h_scales,
            "x_words": x_words, "x_scales": x_scales,
            "coul": bf(np.random.uniform(0.5, 2.0, A)),
            "n0": bf(np.random.standard_normal((R, P)))}


def reference(d, b, gap, h_words, h_scales, x_words, x_scales, coul, n0):
    scaled = f64(b) / f64(gap)
    chi = mxq(f64(d), 1, "e4m3") @ mxq(scaled, 1, "e4m3").T
    trial = unpack4(h_words, h_scales).T @ unpack4(x_words, x_scales)
    pot = trial * f64(coul)[:, None]
    induced = mxq(chi, 1, "e4m3") @ mxq(pot, 0, "e4m3")
    return f64(n0) - induced

from contextlib import ExitStack

import concourse.mybir as mybir
from concourse.masks import make_identity

R, T, A, F, P = 1536, 2048, 1024, 1536, 512
FLOPS = 2 * (R * T * A + F * A * P + R * A * P)

F32 = mybir.dt.float32
BF16 = mybir.dt.bfloat16
U32 = mybir.dt.uint32
I32 = mybir.dt.int32
U8 = mybir.dt.uint8
FP8X4 = mybir.dt.float8_e4m3fn_x4
FP4X4 = mybir.dt.float4_e2m1fn_x4
ALU = mybir.AluOpType

NJ = T // 512
NF = F // 512
NG = A // 512
NB = A // 128
NP = R // 256


def tile_rpa_density_step_s12_kernel(tc, d, b, gap, h_words, h_scales, x_words, x_scales, coul, n0, out):
    nc = tc.nc
    with ExitStack() as ctx:
        keep = ctx.enter_context(tc.tile_pool(name="keep", bufs=1))
        braw = ctx.enter_context(tc.tile_pool(name="braw", bufs=5))
        draw = ctx.enter_context(tc.tile_pool(name="draw", bufs=5))
        work = ctx.enter_context(tc.tile_pool(name="work", bufs=3))
        work2 = ctx.enter_context(tc.tile_pool(name="work2", bufs=2))
        work4 = ctx.enter_context(tc.tile_pool(name="work4", bufs=4))
        trp = ctx.enter_context(tc.psum_pool(name="trp", bufs=4))
        mmp = ctx.enter_context(tc.psum_pool(name="mmp", bufs=4))

        ident = keep.tile([128, 128], F32, name="ident")
        consts = keep.tile([128, 512], BF16, name="consts", align_bytes=64)
        ginv = keep.tile([128, NJ, 2, 2], F32, name="ginv")
        coulp = keep.tile([128, NG, 2, 2], F32, name="coulp")
        x_w = keep.tile([128, NF, 2 * P], U8, name="x_w", align_bytes=64)
        x_s = keep.tile([128, NF, P], U8, name="x_s", align_bytes=64)
        h_w = keep.tile([128, NF, 2 * A], U8, name="h_w", align_bytes=64)
        h_s = keep.tile([128, NF, A], U8, name="h_s", align_bytes=64)
        trial = [keep.tile([128, NG, 4, 128], F32, name=f"trial{m}") for m in range(4)]
        bcodes = [keep.tile([128, NJ * 128], U32, name=f"bcodes{i}", align_bytes=64) for i in range(NB)]
        bscale = [keep.tile([128, NJ * 128], U8, name=f"bscale{i}", align_bytes=64) for i in range(NB)]
        pcodes = [keep.tile([128, P], U32, name=f"pcodes{g}", align_bytes=64) for g in range(NG)]
        pscale = [keep.tile([128, P], U8, name=f"pscale{g}", align_bytes=64) for g in range(NG)]
        ccodes = [[keep.tile([128, 256], U32, name=f"ccodes{q}_{g}", align_bytes=64) for g in range(NG)] for q in range(NP)]
        cscale = [[keep.tile([128, 256], U8, name=f"cscale{q}_{g}", align_bytes=64) for g in range(NG)] for q in range(NP)]
        n0_sb = [keep.tile([128, 4, P], BF16, name=f"n0_{c}") for c in range(3)]

        b_rows = b.rearrange("(g p t) k -> g t p k", p=128, t=4)
        b_sb, d_sb, d_perm, bT, dT, dcodes, dscale, pot, chi = {}, {}, {}, {}, {}, {}, {}, {}, {}
        tr_b, tr_d, tr_p, ps_c, ps_o, ps_t = {}, {}, {}, {}, {}, {}

        def load_b(i):
            b_sb[i] = braw.tile([128, T], BF16, name="b_sb")
            nc.sync.dma_start(out=b_sb[i][:], in_=b_rows[i // 4, i % 4])

        def load_d(r):
            d_sb[r] = draw.tile([128, T], BF16, name="d_sb")
            nc.sync.dma_start(out=d_sb[r][:], in_=d[r * 128 : (r + 1) * 128, :])

        def load_n0(c):
            nc.sync.dma_start(out=n0_sb[c][:], in_=n0[c * 512 : (c + 1) * 512, :].rearrange("(c p) n -> p c n", p=128))

        def prep_b(i):
            for h in range(2):
                tr = trp.tile([128, 4, 128], F32, name="tr")
                tr_b[i, h] = tr
                words = b_sb[i][:].bitcast(F32)
                for s in range(4):
                    j, u = 2 * h + s // 2, s % 2
                    nc.tensor.transpose(tr[:, s, :], words[:, 256 * j + u : 256 * (j + 1) : 2], ident[:])

        def evict_b(i):
            bT[i] = work.tile([128, NJ, 128, 2, 2], BF16, name="bT", align_bytes=64)
            for j in range(NJ):
                src = tr_b[i, j // 2][:, 2 * (j % 2) : 2 * (j % 2) + 2, :].bitcast(BF16).rearrange("p u (a e) -> p a u e", e=2)
                nc.vector.tensor_tensor(
                    out=bT[i][:, j],
                    in0=src,
                    in1=ginv[:, j].unsqueeze(1).to_broadcast([128, 128, 2, 2]),
                    op=ALU.mult,
                )

        def quant_b(i):
            nc.vector.quantize_mx(out=bcodes[i][:].bitcast(FP8X4), scales=bscale[i][:], in_=bT[i][:].rearrange("p j a u e -> p (j a u e)"))

        def mul_t(k):
            half, m = k // 4, k % 4
            ps = mmp.tile([128, 512], F32, name="mm")
            ps_t[k] = ps
            for j in range(NF):
                nc.tensor.matmul_mx(
                    out=ps[:],
                    lhsT=x_w[:, j, 256 * m : 256 * (m + 1)].bitcast(FP4X4),
                    lhsT_scale=x_s[:, j, 128 * m : 128 * (m + 1)],
                    rhs=h_w[:, j, 1024 * half : 1024 * (half + 1)].bitcast(FP4X4),
                    rhs_scale=h_s[:, j, 512 * half : 512 * (half + 1)],
                    start=(j == 0),
                    stop=(j == NF - 1),
                )

        def evict_t(k):
            half, m = k // 4, k % 4
            nc.scalar.copy(out=trial[m][:, half], in_=ps_t[k][:].rearrange("p (a t) -> p t a", t=4))

        def prep_p(k):
            g, m = k // 4, k % 4
            tr = trp.tile([128, 4, 128], F32, name="tr")
            tr_p[k] = tr
            for t in range(4):
                nc.tensor.transpose(tr[:, t, :], trial[m][:, g, t, :], ident[:])

        def evict_p(k):
            g, m = k // 4, k % 4
            if m == 0:
                pot[g] = work2.tile([128, P, 4], BF16, name="pot", align_bytes=64)
            nc.vector.tensor_tensor(
                out=pot[g][:, 128 * m : 128 * (m + 1), :],
                in0=tr_p[k][:].rearrange("p t n -> p n t"),
                in1=coulp[:, g].rearrange("p u e -> p (u e)").unsqueeze(1).to_broadcast([128, 128, 4]),
                op=ALU.mult,
            )

        def quant_p(g):
            nc.vector.quantize_mx(out=pcodes[g][:].bitcast(FP8X4), scales=pscale[g][:], in_=pot[g][:].rearrange("p n t -> p (n t)"))

        def perm_d(r, eng):
            d_perm[r] = work.tile([128, 2, T // 4], F32, name="d_perm")
            src = d_sb[r][:].bitcast(F32).rearrange("p (w u) -> p u w", u=2)
            if eng == "S":
                nc.scalar.copy(out=d_perm[r][:], in_=src)
            else:
                nc.vector.tensor_copy(out=d_perm[r][:], in_=src)

        def prep_d(q):
            for r in (2 * q, 2 * q + 1):
                for h in range(2):
                    tr = trp.tile([128, 4, 128], F32, name="tr")
                    tr_d[r, h] = tr
                    for s in range(4):
                        j, u = 2 * h + s // 2, s % 2
                        nc.tensor.transpose(tr[:, s, :], d_perm[r][:, u, 128 * j : 128 * (j + 1)], ident[:])

        def evict_d(q, engs):
            dT[q] = work2.tile([128, NJ, 256, 2], F32, name="dT", align_bytes=64)
            for r in (2 * q, 2 * q + 1):
                for h in range(2):
                    dst = dT[q][:, 2 * h : 2 * h + 2, 128 * (r % 2) : 128 * (r % 2) + 128, :]
                    src = tr_d[r, h][:].rearrange("p (j u) a -> p j a u", u=2)
                    if engs[2 * (r % 2) + h] == "S":
                        nc.scalar.copy(out=dst, in_=src)
                    else:
                        nc.vector.tensor_copy(out=dst, in_=src)

        def quant_d(q):
            dcodes[q] = work4.tile([128, NJ, 256], U32, name="dcodes", align_bytes=64)
            dscale[q] = work4.tile([128, NJ, 256], U8, name="dscale", align_bytes=64)
            for h in range(2):
                nc.vector.quantize_mx(
                    out=dcodes[q][:, 2 * h : 2 * h + 2].rearrange("p j a -> p (j a)").bitcast(FP8X4),
                    scales=dscale[q][:, 2 * h : 2 * h + 2].rearrange("p j a -> p (j a)"),
                    in_=dT[q][:, 2 * h : 2 * h + 2].rearrange("p j a u -> p (j a u)").bitcast(BF16),
                )

        def mul_c(q, g):
            for tp in range(2):
                ps = mmp.tile([128, 2, 256], F32, name="mm")
                ps_c[q, g, tp] = ps
                for e in range(2):
                    i = 4 * g + 2 * tp + e
                    for j in range(NJ):
                        nc.tensor.matmul_mx(
                            out=ps[:, e, :],
                            lhsT=bcodes[i][:, 128 * j : 128 * (j + 1)].bitcast(FP8X4),
                            lhsT_scale=bscale[i][:, 128 * j : 128 * (j + 1)],
                            rhs=dcodes[q][:, j, :].bitcast(FP8X4),
                            rhs_scale=dscale[q][:, j, :],
                            start=(j == 0),
                            stop=(j == NJ - 1),
                        )

        def evict_c(q, g, engs):
            chi[q, g] = work4.tile([128, 256, 4], BF16, name="chi", align_bytes=64)
            for tp in range(2):
                dst = chi[q, g][:, :, 2 * tp : 2 * tp + 2]
                src = ps_c[q, g, tp][:].rearrange("p e a -> p a e")
                if engs[tp] == "S":
                    nc.scalar.copy(out=dst, in_=src)
                else:
                    nc.vector.tensor_copy(out=dst, in_=src)

        def quant_c(q, g):
            nc.vector.quantize_mx(out=ccodes[q][g][:].bitcast(FP8X4), scales=cscale[q][g][:], in_=chi[q, g][:].rearrange("p a t -> p (a t)"))

        def mul_o(q):
            for r in (2 * q, 2 * q + 1):
                ps = mmp.tile([128, 512], F32, name="mm")
                ps_o[r] = ps
                cols = slice(128 * (r % 2), 128 * (r % 2) + 128)
                for g in range(NG):
                    nc.tensor.matmul_mx(
                        out=ps[:],
                        lhsT=ccodes[q][g][:, cols].bitcast(FP8X4),
                        lhsT_scale=cscale[q][g][:, cols],
                        rhs=pcodes[g][:].bitcast(FP8X4),
                        rhs_scale=pscale[g][:],
                        start=(g == 0),
                        stop=(g == NG - 1),
                    )

        def evict_o(q):
            for r in (2 * q, 2 * q + 1):
                res = work4.tile([128, P], F32, name="res")
                nc.vector.tensor_tensor(out=res[:], in0=n0_sb[r // 4][:, r % 4, :], in1=ps_o[r][:], op=ALU.subtract)
                nc.sync.dma_start(out=out[r * 128 : (r + 1) * 128, :], in_=res[:])

        with tc.manual_schedule():
            nc.vector.memset(consts[:], 0.0)
            nc.scalar.dma_start(out=consts[0:4, :], in_=gap.rearrange("(j k) -> j k", k=512))
            nc.scalar.dma_start(out=consts[4:6, :], in_=coul.rearrange("(j k) -> j k", k=512))
            load_b(0)
            load_b(1)
            make_identity(nc, ident[:])
            nc.vector.memset(x_s[:].rearrange("p g n -> p (g n)").bitcast(I32), 0)
            nc.vector.memset(h_s[:].rearrange("p g n -> p (g n)").bitcast(I32), 0)
            for q in range(4):
                nc.scalar.dma_start(out=x_s[32 * q : 32 * q + 4].bitcast(I32), in_=x_scales.bitcast(I32)[:, 4 * q : 4 * q + 4, :].rearrange("g q n -> q g n"))
                nc.scalar.dma_start(out=h_s[32 * q : 32 * q + 4].bitcast(I32), in_=h_scales.bitcast(I32)[:, 4 * q : 4 * q + 4, :].rearrange("g q n -> q g n"))
            nc.sync.dma_start(out=x_w[:].bitcast(I32), in_=x_words.bitcast(I32).rearrange("g p n -> p g n"))
            nc.sync.dma_start(out=h_w[:].bitcast(I32), in_=h_words.bitcast(I32).rearrange("g p n -> p g n"))
            for i in (2, 3):
                load_b(i)
            for r in (0, 1):
                load_d(r)
            for i in (4, 5):
                load_b(i)
            for r in (2, 3):
                load_d(r)
            for i in (6, 7):
                load_b(i)
            for r in range(4, 12):
                load_d(r)
                if r % 4 == 3 or r == 5:
                    load_n0({5: 0, 7: 1, 11: 2}[r])

            prep_b(0)
            trc = trp.tile([128, 4, 128], F32, name="tr")
            for u in range(2):
                nc.tensor.transpose(trc[:, u, :], consts[:].bitcast(F32)[:, u : 256 : 2], ident[:])
            cview = trc[:, 0:2, :].bitcast(BF16)
            nc.vector.reciprocal(out=ginv[:].rearrange("p j u e -> p u j e"), in_=cview[:, :, 0:8].rearrange("p u (j e) -> p u j e", e=2))
            nc.vector.tensor_copy(out=coulp[:].rearrange("p j u e -> p u j e"), in_=cview[:, :, 8:12].rearrange("p u (j e) -> p u j e", e=2))
            prep_b(1)
            evict_b(0)
            evict_b(1)
            quant_b(0)
            for k in range(4):
                mul_t(k)
                evict_t(k)
            prep_b(2)
            evict_b(2)
            quant_b(1)
            for k in range(4, 8):
                mul_t(k)
                evict_t(k)
            perm_d(0, "S")
            perm_d(1, "S")
            prep_b(3)
            evict_b(3)
            quant_b(2)
            prep_d(0)
            evict_d(0, "SSSS")
            quant_b(3)
            prep_b(4)
            perm_d(2, "S")
            quant_d(0)
            evict_b(4)
            mul_c(0, 0)
            perm_d(3, "S")
            prep_b(5)
            evict_b(5)
            quant_b(4)
            evict_c(0, 0, "SS")
            prep_d(1)
            evict_d(1, "SSSS")
            quant_b(5)
            quant_c(0, 0)
            quant_d(1)
            mul_c(1, 0)
            prep_b(6)
            evict_b(6)
            perm_d(4, "S")
            evict_c(1, 0, "SS")
            perm_d(5, "S")
            prep_b(7)
            evict_b(7)
            quant_b(6)
            quant_b(7)
            quant_c(1, 0)
            prep_d(2)
            evict_d(2, "SSSS")
            quant_d(2)
            mul_c(0, 1)
            evict_c(0, 1, "SS")
            for k in range(4):
                prep_p(k)
                evict_p(k)
            mul_c(1, 1)
            evict_c(1, 1, "SS")
            quant_p(0)
            quant_c(0, 1)
            for k in range(4, 8):
                prep_p(k)
                evict_p(k)
            perm_d(6, "V")
            perm_d(7, "V")
            mul_c(2, 0)
            quant_p(1)
            quant_c(1, 1)
            evict_c(2, 0, "SS")
            prep_d(3)
            evict_d(3, "SSSS")
            mul_o(0)
            mul_c(2, 1)
            evict_o(0)
            quant_c(2, 0)
            quant_d(3)
            evict_c(2, 1, "SS")
            mul_o(1)
            for q in range(3, NP):
                if q + 1 < NP:
                    perm_d(2 * q + 2, "V")
                    perm_d(2 * q + 3, "V")
                mul_c(q, 0)
                quant_c(q - 1, 1)
                evict_o(q - 2)
                evict_c(q, 0, "SV")
                if q + 1 < NP:
                    prep_d(q + 1)
                    evict_d(q + 1, "SSSS")
                mul_c(q, 1)
                quant_c(q, 0)
                if q + 1 < NP:
                    quant_d(q + 1)
                mul_o(q - 1)
                evict_c(q, 1, "SV")
            evict_o(NP - 2)
            quant_c(NP - 1, 1)
            mul_o(NP - 1)
            evict_o(NP - 1)
